import numpy as np, ml_dtypes
CORES = [73,201,329,457,330]
N = 5
import mx_ref
NC = 512
BF = ml_dtypes.bfloat16
def setup_inputs(rng):
    def f(*shape):
        return mx_ref.flush((rng.standard_normal(shape, dtype=np.float32) * np.exp2(rng.integers(-2, 3, shape[:-1] + (1,)))).astype(BF))
    return {"x": f(N, 128, 512), "w": f(N, 128, 4 * NC)}
def setup_inputs_blocks(rng):
    d = setup_inputs(rng)
    for k in ("x", "w"): d[k] = mx_ref.spread(d[k], rng, 4)
    return d
def setup_inputs_wide(rng):
    d = setup_inputs(rng)
    for k in ("x", "w"): d[k] = mx_ref.flush((d[k].astype(np.float32) * np.exp2(rng.integers(-6, 7, (N, 1, 1))).astype(np.float32)).astype(BF))
    return d
def setup_inputs_near(rng):
    d = setup_inputs(rng); v = d["w"].astype(np.float32).reshape(N, 128, -1, 4)
    d["w"] = mx_ref.flush((v[:1, :, :1] + v / 64).reshape(d["w"].shape).astype(BF))
    return d
def setup_inputs_twins(rng):
    d = setup_inputs(rng); v = d["w"].reshape(N, 128, -1, 4).copy(); a, b = rng.permutation(N)[:2]; i, j, k = rng.integers(0, v.shape[2], 3)
    v[a, :, i] = (v[a, :, i].astype(np.float32) * 8).astype(BF); v[a, :, j] = v[a, :, i]; v[b, :, k] = v[a, :, i]
    d["w"] = v.reshape(d["w"].shape)
    return d
def reference(x, w):
    W = [mx_ref.quantize(w[r]) for r in range(N)]
    y = np.zeros((N, 128, 2), np.float32)
    for j in range(N):
        X = mx_ref.quantize(x[j])
        L = np.concatenate([mx_ref.matmul(X, W[r]) for r in range(N)], axis=1)
        y[j][:, 0] = L.max(axis=1); y[j][:, 1] = L.argmax(axis=1)
    return {"y": y}

@@ -1,0 +1,258 @@
+from concourse.bass import DstId, RemoteDMATransfer
+from concourse.mybir import dt, AluOpType, AxisListType, ActivationFunctionType
+
+N = 5
+NC = 512
+TOK = 128
+PITCH = NC + 4
+LOW = -1.0e29
+
+SCRATCH = {
+    "xb": ("sbuf", [128, 4 * TOK], "bfloat16"),
+    "wb": ("sbuf", [128, 4 * NC], "bfloat16"),
+    "xq": ("sbuf", [128, N * TOK], "float8_e4m3fn_x4"),
+    "xs": ("sbuf", [128, N * TOK], "uint8"),
+    "wq": ("sbuf", [128, NC], "float8_e4m3fn_x4"),
+    "ws": ("sbuf", [128, NC], "uint8"),
+    "ps": ("psum", [128, N * NC], "float32"),
+    "low": ("sbuf", [128, NC], "bfloat16"),
+    "pm": ("sbuf", [128, N * PITCH], "float32"),
+    "sgn": ("sbuf", [128, N * NC], "bfloat16"),
+    "off": ("sbuf", [128, 8], "float32"),
+    "res": ("sbuf", [128, 4 * N], "float32"),
+    "fwd": ("sbuf", [128, 8], "float32"),
+    "idx": ("sbuf", [128, 8], "float32"),
+    "neq": ("sbuf", [128, 8], "float32"),
+    "fin": ("sbuf", [128, 12], "float32"),
+}
+SEMAPHORES = (["ldx", "ldw", "qx", "qw", "low", "off", "sent", "got", "own", "m0", "m1", "m2", "done", "stored"]
+              + ["x%d" % j for j in range(N)] + ["mm%d" % j for j in range(N)] + ["sc%d" % j for j in range(N)]
+              + ["sg%d" % j for j in range(N)] + ["f%d" % j for j in range(2)])
+
+
+def _bits(mask):
+    return [1 << b for b in range(mask.bit_length()) if mask >> b & 1]
+
+
+def _plan(C, topo):
+    R = range(N)
+    may = lambda a, b: topo.may_write(C[a], C[b])
+    chip = lambda a: (topo.host(C[a]), topo.chip(C[a]))
+    rack = lambda a: topo.rack(topo.host(C[a]))
+    P = {"far": [], "lead": [], "rest": [], "mates": [], "entry": [], "pass": [], "via": {}}
+    for j in R:
+        far = [r for r in R if r != j and not may(j, r)]
+        over = [r for r in R if rack(r) != rack(j) and may(j, r)]
+        near = {}
+        for r in R:
+            if rack(r) == rack(j) and chip(r) != chip(j):
+                near.setdefault(chip(r), []).append(r)
+        P["far"].append(far)
+        P["lead"].append(over[0])
+        P["rest"].append([r for r in over[1:] if chip(r) == chip(over[0])])
+        P["mates"].append([r for r in R if r != j and chip(r) == chip(j)])
+        P["entry"].append([v[-1] for v in near.values()])
+        P["pass"].append({v[-1]: v[:-1] for v in near.values() if len(v) > 1})
+    P["order"] = sorted(R, key=lambda j: (P["lead"][j], j))
+    load = [0] * N
+    for j in R:
+        for r in P["far"][j]:
+            v = min([v for v in R if may(r, v) and may(v, j) and v not in (j, r)], key=lambda v: (load[v], -v))
+            load[v] += 1
+            P["via"][j, r] = v
+    return P
+
+
+def rank_program(g, core, T, topo):
+    me = T.rank_of(core)
+    if me is None:
+        return
+    C = T.cores
+    P = _plan(C, topo)
+    slot = {j: s for s, j in enumerate(P["order"])}
+    S = T.sem
+    f32max = AluOpType.max
+
+    def off_chip(r):
+        others = [d for d in range(N) if d != r and topo.may_write(C[r], C[d])
+                  and (topo.host(C[d]), topo.chip(C[d])) != (topo.host(C[r]), topo.chip(C[r]))]
+        m = 0xFFFFFFFF
+        for d in others:
+            m &= topo.mask(C[r], C[d])
+        return m
+
+    def engines(r, d):
+        m = topo.mask(C[r], C[d])
+        return _bits(m & ~off_chip(r)) if d in P["mates"][r] else _bits(m & off_chip(r))
+
+    group = {}
+    for j in P["order"]:
+        group.setdefault((P["lead"][j], tuple(P["far"][j])), []).append(j)
+    arrive = {}
+    for j in range(N):
+        for d in [P["lead"][j]] + P["entry"][j] + P["mates"][j]:
+            arrive[d, j] = ("x%d" % j, 2 * len(engines(j, d)))
+        for d in P["rest"][j]:
+            arrive[d, j] = ("x%d" % j, 2 * len(engines(P["lead"][j], d)))
+        for e, ds in P["pass"][j].items():
+            for d in ds:
+                arrive[d, j] = ("x%d" % j, 2 * len(engines(e, d)))
+    for (lead, far), tiles in group.items():
+        for d in far:
+            for j in tiles:
+                arrive[d, j] = ("x%d" % tiles[0], 2 * len(engines(lead, d)))
+
+    sent = [0]
+
+    def send(parts):
+        for p in parts:
+            sent[0] += len(p[1])
+        if len(parts) == 1 and len(parts[0][0]) == 1:
+            (d,), e, src, dst, sem = parts[0]
+            rid, pid = topo.addr(C[d], core)
+            g.remote_dma(dst, src, S[sem], S["sent"], pid, rid, sum(e))
+            return
+        tr = []
+        for ds, e, src, dst, sem in parts:
+            ids = [DstId(rid=a[0], pnc=a[1]) for a in (topo.addr(C[d], core) for d in ds)]
+            tr.append(RemoteDMATransfer(dst_ids=ids, dma_engine_mask=sum(e), remote_sem=S[sem],
+                                        srcs=[src], dsts=[dst] * len(ds)))
+        g.remote_dma_fused(tr, local_sem=S["sent"])
+
+    def send_tiles(tiles, dests):
+        a = min(slot[j] for j in tiles) * TOK
+        b = a + len(tiles) * TOK
+        mates = [d for d in dests if d in P["mates"][me]]
+        away = [d for d in dests if d not in mates]
+        for v in (T.xq[:, a:b].bitcast(dt.uint8), T.xs[:, a:b]):
+            send([(ds, engines(me, ds[0]), v, v, "x%d" % tiles[0]) for ds in (away, mates) if ds])
+
+    def kind(r, j):
+        if j == r:
+            return 0
+        if P["lead"][j] == r:
+            return 1
+        if r in P["entry"][j] or r in P["mates"][j]:
+            return 2
+        return 3 if r in P["far"][j] else 4
+
+    tiles = sorted(range(N), key=lambda j: (kind(me, j), j))
+
+    def xcols(j):
+        return slice(slot[j] * TOK, (slot[j] + 1) * TOK)
+
+    g.sync.dma_start(T.xb[:], T.x[:]).then_inc(S["ldx"], 16)
+    g.sync.dma_start(T.wb[:], T.w[:]).then_inc(S["ldw"], 16)
+
+    g.vector.memset(T.low[:], LOW).then_inc(S["low"], 1)
+    g.vector.wait_ge(S["ldx"], 16)
+    g.vector.quantize_mx(T.xq[:, xcols(me)], T.xs[:, xcols(me)], T.xb[:]).then_inc(S["qx"], 1)
+    g.vector.wait_ge(S["ldw"], 16)
+    g.vector.quantize_mx(T.wq[:], T.ws[:], T.wb[:]).then_inc(S["qw"], 1)
+    g.vector.wait_ge(S["low"], 1)
+
+    g.tensor.wait_ge(S["qx"], 1)
+    g.tensor.wait_ge(S["qw"], 1)
+    seen = set()
+    for j in tiles:
+        if j != me and arrive[me, j][0] not in seen:
+            seen.add(arrive[me, j][0])
+            g.tensor.wait_ge(S[arrive[me, j][0]], arrive[me, j][1])
+        bank = T.ps[:, j * NC:(j + 1) * NC]
+        g.tensor.matmul_mx(bank, T.xq[:, xcols(j)], T.xs[:, xcols(j)], T.wq[:], T.ws[:], True, True).then_inc(S["mm%d" % j], 1)
+        a = j * PITCH
+        g.vector.wait_ge(S["mm%d" % j], 1)
+        g.vector.tensor_tensor_scan(T.pm[:, a:a + NC], bank, T.low[:], LOW, f32max, f32max).then_inc(S["sc%d" % j], 1)
+        g.scalar.wait_ge(S["sc%d" % j], 1)
+        g.scalar.activation(T.sgn[:, j * NC:(j + 1) * NC], T.pm[:, a:a + NC], ActivationFunctionType.Sign,
+                            bias=T.pm[:, a + NC - 1:a + NC], scale=-1.0,
+                            accum_out=T.pm[:, a + NC:a + NC + 1]).then_inc(S["sg%d" % j], 1)
+
+    def pair(j):
+        return T.pm[:, j * PITCH + NC - 1:j * PITCH + NC + 1]
+
+    def place(r):
+        return T.res[:, 4 * (N - 1 - r):4 * (N - 1 - r) + 2]
+
+    g.iota(T.off[:, 0:N], [[-NC, N]], (N - 1) * NC, 0, allow_small_or_imprecise_dtypes=True).then_inc(S["off"], 1)
+    g.wait_ge(S["qx"], 1)
+    send_tiles([me], [P["lead"][me]])
+    send_tiles([me], P["entry"][me] + P["mates"][me])
+    for (lead, far), ts in group.items():
+        if lead == me:
+            for j in ts:
+                g.wait_ge(S[arrive[me, j][0]], arrive[me, j][1])
+            send_tiles(ts, list(far) + P["rest"][ts[0]])
+    for j in range(N):
+        if me in P["pass"][j]:
+            g.wait_ge(S[arrive[me, j][0]], arrive[me, j][1])
+            send_tiles([j], P["pass"][j][me])
+
+    def results(r, k):
+        return [j for j in range(N) if kind(r, j) == k]
+
+    def share(r, js):
+        mates = [j for j in js if j in P["mates"][r]]
+        away = [j for j in js if j not in mates]
+        out = {}
+        for part in (mates, away):
+            if part:
+                e = engines(r, part[0])
+                n = len(e)
+                while n * len(part) > len(e):
+                    n //= 2
+                for i, j in enumerate(part):
+                    out[j] = e[i * n:(i + 1) * n]
+        return out
+
+    def direct(k):
+        js = results(me, k)
+        if js:
+            for j in js:
+                g.wait_ge(S["sg%d" % j], 1)
+            e = share(me, js)
+            send([([j], e[j], pair(j), place(me), "got") for j in js])
+
+    relays = {}
+    for (j, r), v in sorted(P["via"].items(), key=lambda kv: (kv[0][1], kv[0][0])):
+        relays.setdefault(v, []).append((r, j))
+
+    direct(1)
+    direct(2)
+    for j in results(me, 3):
+        v = P["via"][j, me]
+        i = relays[v].index((me, j))
+        g.wait_ge(S["sg%d" % j], 1)
+        send([([v], engines(me, v), pair(j), T.fwd[:, 4 * i:4 * i + 2], "f%d" % i)])
+    direct(4)
+    for i, (r, j) in enumerate(relays.get(me, [])):
+        g.wait_ge(S["f%d" % i], len(engines(r, me)))
+        send([([j], engines(me, j), T.fwd[:, 4 * i:4 * i + 2], place(r), "got")])
+    g.wait_ge(S["sent"], sent[0])
+
+    got = 0
+    for r in range(N):
+        if r != me:
+            k = kind(r, me)
+            if k == 3:
+                got += len(engines(P["via"][me, r], me))
+            else:
+                got += len(share(r, results(r, k))[me])
+    vals = T.res[:, 0:4 * N:4]
+    cols = T.res[:, 1:4 * N:4]
+    v = g.vector
+    v.wait_ge(S["sg%d" % me], 1)
+    v.tensor_copy(place(me), pair(me)).then_inc(S["own"], 1)
+    v.wait_ge(S["off"], 1)
+    v.wait_ge(S["own"], 1)
+    v.wait_ge(S["got"], got)
+    v.tensor_reduce(T.fin[:, 7:8], vals, AxisListType.X, f32max).then_inc(S["m0"], 1)
+    v.tensor_tensor(T.idx[:, 0:N], cols, T.off[:, 0:N], AluOpType.add).then_inc(S["m1"], 1)
+    v.wait_ge(S["m0"], 1)
+    v.tensor_scalar(T.neq[:, 0:N], vals, T.fin[:, 7:8], None, AluOpType.is_lt).then_inc(S["m2"], 1)
+    v.wait_ge(S["m1"], 1)
+    v.wait_ge(S["m2"], 1)
+    v.tensor_tensor_scan(T.fin[:, 0:10:2], T.neq[:, 0:N], T.idx[:, 0:N], 0.0, AluOpType.mult, f32max).then_inc(S["done"], 1)
+    g.sync.wait_ge(S["done"], 1)
+    g.sync.dma_start(T.y[:], T.fin[:, 7:9]).then_inc(S["stored"], 16)
+    g.sync.wait_ge(S["stored"], 16)

@@ -3,6 +3,8 @@ from concourse.mybir import dt, AluOpType, AxisListType, ActivationFunctionType
 
 N = 5
 NC = 512
+HALF = NC // 2
+WHOLE = 3
 TOK = 128
 PITCH = NC + 4
 LOW = -1.0e29
@@ -14,7 +16,7 @@ SCRATCH = {
     "xs": ("sbuf", [128, N * TOK], "uint8"),
     "wq": ("sbuf", [128, NC], "float8_e4m3fn_x4"),
     "ws": ("sbuf", [128, NC], "uint8"),
-    "ps": ("psum", [128, N * NC], "float32"),
+    "ps": ("psum", [128, (2 * N - WHOLE) * NC], "float32"),
     "low": ("sbuf", [128, NC], "bfloat16"),
     "pm": ("sbuf", [128, N * PITCH], "float32"),
     "sgn": ("sbuf", [128, N * NC], "bfloat16"),
@@ -26,8 +28,7 @@ SCRATCH = {
     "fin": ("sbuf", [128, 12], "float32"),
 }
 SEMAPHORES = (["ldx", "ldw", "qx", "qw", "low", "off", "sent", "got", "own", "m0", "m1", "m2", "done", "stored"]
-              + ["x%d" % j for j in range(N)] + ["mm%d" % j for j in range(N)] + ["sc%d" % j for j in range(N)]
-              + ["sg%d" % j for j in range(N)] + ["f%d" % j for j in range(2)])
+              + [k + str(j) for k in ("q", "s", "ma", "mb", "sa", "sb", "sg") for j in range(N)] + ["f0", "f1"])
 
 
 def _bits(mask):
@@ -41,25 +42,21 @@ def _plan(C, topo):
     rack = lambda a: topo.rack(topo.host(C[a]))
     P = {"far": [], "lead": [], "rest": [], "mates": [], "entry": [], "pass": [], "via": {}}
     for j in R:
-        far = [r for r in R if r != j and not may(j, r)]
         over = [r for r in R if rack(r) != rack(j) and may(j, r)]
         near = {}
         for r in R:
             if rack(r) == rack(j) and chip(r) != chip(j):
                 near.setdefault(chip(r), []).append(r)
-        P["far"].append(far)
+        P["far"].append([r for r in R if r != j and not may(j, r)])
         P["lead"].append(over[0])
         P["rest"].append([r for r in over[1:] if chip(r) == chip(over[0])])
         P["mates"].append([r for r in R if r != j and chip(r) == chip(j)])
         P["entry"].append([v[-1] for v in near.values()])
         P["pass"].append({v[-1]: v[:-1] for v in near.values() if len(v) > 1})
-    P["order"] = sorted(R, key=lambda j: (P["lead"][j], j))
-    load = [0] * N
-    for j in R:
         for r in P["far"][j]:
-            v = min([v for v in R if may(r, v) and may(v, j) and v not in (j, r)], key=lambda v: (load[v], -v))
-            load[v] += 1
-            P["via"][j, r] = v
+            P["via"][j, r] = over[0]
+    P["led"] = [[j for j in R if P["lead"][j] == d] for d in R]
+    P["order"] = sorted(R, key=lambda j: (P["lead"][j], j))
     return P
 
 
@@ -72,35 +69,39 @@ def rank_program(g, core, T, topo):
     slot = {j: s for s, j in enumerate(P["order"])}
     S = T.sem
     f32max = AluOpType.max
+    chip = lambda r: (topo.host(C[r]), topo.chip(C[r]))
+    lead, far, rest, mates, entry, passed = (P[k] for k in ("lead", "far", "rest", "mates", "entry", "pass"))
 
-    def off_chip(r):
-        others = [d for d in range(N) if d != r and topo.may_write(C[r], C[d])
-                  and (topo.host(C[d]), topo.chip(C[d])) != (topo.host(C[r]), topo.chip(C[r]))]
-        m = 0xFFFFFFFF
-        for d in others:
-            m &= topo.mask(C[r], C[d])
-        return m
+    def engines(a, b, use="all"):
+        off = 0xFFFFFFFF
+        for d in range(N):
+            if d != a and chip(d) != chip(a) and topo.may_write(C[a], C[d]):
+                off &= topo.mask(C[a], C[d])
+        m = topo.mask(C[a], C[b])
+        e = _bits(m & ~off if chip(a) == chip(b) else m & off)
+        return {"all": e, "A": e[0::2], "B": e[1::2]}[use]
 
-    def engines(r, d):
-        m = topo.mask(C[r], C[d])
-        return _bits(m & ~off_chip(r)) if d in P["mates"][r] else _bits(m & off_chip(r))
+    def tile_calls(n):
+        out = [("s", [n], [lead[n]], "A"), ("q", [n], [lead[n]], "A"),
+               ("s", [n], entry[n] + mates[n], "B"), ("q", [n], entry[n] + mates[n], "B")]
+        groups = {}
+        for j in P["order"]:
+            if lead[j] == n:
+                groups.setdefault(tuple(far[j] + rest[j]), []).append(j)
+        for ds, ts in groups.items():
+            out.append(("s", ts, list(ds), "all"))
+            out += [("q", [j], list(ds), "all") for j in ts]
+        for j in range(N):
+            if n in passed[j]:
+                out += [("s", [j], passed[j][n], "all"), ("q", [j], passed[j][n], "all")]
+        return out
 
-    group = {}
-    for j in P["order"]:
-        group.setdefault((P["lead"][j], tuple(P["far"][j])), []).append(j)
     arrive = {}
-    for j in range(N):
-        for d in [P["lead"][j]] + P["entry"][j] + P["mates"][j]:
-            arrive[d, j] = ("x%d" % j, 2 * len(engines(j, d)))
-        for d in P["rest"][j]:
-            arrive[d, j] = ("x%d" % j, 2 * len(engines(P["lead"][j], d)))
-        for e, ds in P["pass"][j].items():
+    for n in range(N):
+        for kind, ts, ds, use in tile_calls(n):
             for d in ds:
-                arrive[d, j] = ("x%d" % j, 2 * len(engines(e, d)))
-    for (lead, far), tiles in group.items():
-        for d in far:
-            for j in tiles:
-                arrive[d, j] = ("x%d" % tiles[0], 2 * len(engines(lead, d)))
+                for j in ts:
+                    arrive[d, kind, j] = (kind + str(ts[0]), len(engines(n, d, use)))
 
     sent = [0]
 
@@ -119,85 +120,39 @@ def rank_program(g, core, T, topo):
                                         srcs=[src], dsts=[dst] * len(ds)))
         g.remote_dma_fused(tr, local_sem=S["sent"])
 
-    def send_tiles(tiles, dests):
-        a = min(slot[j] for j in tiles) * TOK
-        b = a + len(tiles) * TOK
-        mates = [d for d in dests if d in P["mates"][me]]
-        away = [d for d in dests if d not in mates]
-        for v in (T.xq[:, a:b].bitcast(dt.uint8), T.xs[:, a:b]):
-            send([(ds, engines(me, ds[0]), v, v, "x%d" % tiles[0]) for ds in (away, mates) if ds])
+    seen = {"g": set(), "tensor": set()}
 
-    def kind(r, j):
-        if j == r:
-            return 0
-        if P["lead"][j] == r:
-            return 1
-        if r in P["entry"][j] or r in P["mates"][j]:
-            return 2
-        return 3 if r in P["far"][j] else 4
-
-    tiles = sorted(range(N), key=lambda j: (kind(me, j), j))
+    def landed(queue, name, kind, j):
+        if j != me and arrive[me, kind, j][0] not in seen[name]:
+            seen[name].add(arrive[me, kind, j][0])
+            queue.wait_ge(S[arrive[me, kind, j][0]], arrive[me, kind, j][1])
 
     def xcols(j):
         return slice(slot[j] * TOK, (slot[j] + 1) * TOK)
 
-    g.sync.dma_start(T.xb[:], T.x[:]).then_inc(S["ldx"], 16)
-    g.sync.dma_start(T.wb[:], T.w[:]).then_inc(S["ldw"], 16)
-
-    g.vector.memset(T.low[:], LOW).then_inc(S["low"], 1)
-    g.vector.wait_ge(S["ldx"], 16)
-    g.vector.quantize_mx(T.xq[:, xcols(me)], T.xs[:, xcols(me)], T.xb[:]).then_inc(S["qx"], 1)
-    g.vector.wait_ge(S["ldw"], 16)
-    g.vector.quantize_mx(T.wq[:], T.ws[:], T.wb[:]).then_inc(S["qw"], 1)
-    g.vector.wait_ge(S["low"], 1)
-
-    g.tensor.wait_ge(S["qx"], 1)
-    g.tensor.wait_ge(S["qw"], 1)
-    seen = set()
-    for j in tiles:
-        if j != me and arrive[me, j][0] not in seen:
-            seen.add(arrive[me, j][0])
-            g.tensor.wait_ge(S[arrive[me, j][0]], arrive[me, j][1])
-        bank = T.ps[:, j * NC:(j + 1) * NC]
-        g.tensor.matmul_mx(bank, T.xq[:, xcols(j)], T.xs[:, xcols(j)], T.wq[:], T.ws[:], True, True).then_inc(S["mm%d" % j], 1)
-        a = j * PITCH
-        g.vector.wait_ge(S["mm%d" % j], 1)
-        g.vector.tensor_tensor_scan(T.pm[:, a:a + NC], bank, T.low[:], LOW, f32max, f32max).then_inc(S["sc%d" % j], 1)
-        g.scalar.wait_ge(S["sc%d" % j], 1)
-        g.scalar.activation(T.sgn[:, j * NC:(j + 1) * NC], T.pm[:, a:a + NC], ActivationFunctionType.Sign,
-                            bias=T.pm[:, a + NC - 1:a + NC], scale=-1.0,
-                            accum_out=T.pm[:, a + NC:a + NC + 1]).then_inc(S["sg%d" % j], 1)
-
-    def pair(j):
-        return T.pm[:, j * PITCH + NC - 1:j * PITCH + NC + 1]
-
-    def place(r):
-        return T.res[:, 4 * (N - 1 - r):4 * (N - 1 - r) + 2]
-
-    g.iota(T.off[:, 0:N], [[-NC, N]], (N - 1) * NC, 0, allow_small_or_imprecise_dtypes=True).then_inc(S["off"], 1)
-    g.wait_ge(S["qx"], 1)
-    send_tiles([me], [P["lead"][me]])
-    send_tiles([me], P["entry"][me] + P["mates"][me])
-    for (lead, far), ts in group.items():
-        if lead == me:
+    def send_tiles():
+        for kind, ts, ds, use in tile_calls(me):
             for j in ts:
-                g.wait_ge(S[arrive[me, j][0]], arrive[me, j][1])
-            send_tiles(ts, list(far) + P["rest"][ts[0]])
-    for j in range(N):
-        if me in P["pass"][j]:
-            g.wait_ge(S[arrive[me, j][0]], arrive[me, j][1])
-            send_tiles([j], P["pass"][j][me])
+                landed(g, "g", kind, j)
+            a = min(slot[j] for j in ts) * TOK
+            b = a + len(ts) * TOK
+            v = T.xq[:, a:b].bitcast(dt.uint8) if kind == "q" else T.xs[:, a:b]
+            away = [d for d in ds if chip(d) != chip(me)]
+            here = [d for d in ds if chip(d) == chip(me)]
+            send([(part, engines(me, part[0], use), v, v, kind + str(ts[0])) for part in (away, here) if part])
 
-    def results(r, k):
-        return [j for j in range(N) if kind(r, j) == k]
+    def result_calls(r):
+        a = P["led"][r]
+        f = [j for j in range(N) if r in far[j]]
+        return [js for js in [a] + [[j] for j in f] + [[j for j in range(N) if j != r and j not in a + f]] if js]
 
     def share(r, js):
-        mates = [j for j in js if j in P["mates"][r]]
-        away = [j for j in js if j not in mates]
+        hop = {j: P["via"].get((j, r), j) for j in js}
+        here = [j for j in js if chip(hop[j]) == chip(r)]
         out = {}
-        for part in (mates, away):
+        for part in (here, [j for j in js if j not in here]):
             if part:
-                e = engines(r, part[0])
+                e = engines(r, hop[part[0]])
                 n = len(e)
                 while n * len(part) > len(e):
                     n //= 2
@@ -205,42 +160,94 @@ def rank_program(g, core, T, topo):
                     out[j] = e[i * n:(i + 1) * n]
         return out
 
-    def direct(k):
-        js = results(me, k)
-        if js:
-            for j in js:
-                g.wait_ge(S["sg%d" % j], 1)
-            e = share(me, js)
-            send([([j], e[j], pair(j), place(me), "got") for j in js])
-
+    uses = {(r, j): e for r in range(N) for js in result_calls(r) for j, e in share(r, js).items()}
     relays = {}
-    for (j, r), v in sorted(P["via"].items(), key=lambda kv: (kv[0][1], kv[0][0])):
+    for (j, r), v in sorted(P["via"].items()):
         relays.setdefault(v, []).append((r, j))
 
-    direct(1)
-    direct(2)
-    for j in results(me, 3):
-        v = P["via"][j, me]
-        i = relays[v].index((me, j))
-        g.wait_ge(S["sg%d" % j], 1)
-        send([([v], engines(me, v), pair(j), T.fwd[:, 4 * i:4 * i + 2], "f%d" % i)])
-    direct(4)
-    for i, (r, j) in enumerate(relays.get(me, [])):
-        g.wait_ge(S["f%d" % i], len(engines(r, me)))
-        send([([j], engines(me, j), T.fwd[:, 4 * i:4 * i + 2], place(r), "got")])
+    def pair(j):
+        return T.pm[:, j * PITCH + NC - 1:j * PITCH + NC + 1]
+
+    def place(r):
+        return T.res[:, 4 * (N - 1 - r):4 * (N - 1 - r) + 2]
+
+    def send_results():
+        for js in result_calls(me):
+            parts = []
+            for j in js:
+                g.wait_ge(S["sg%d" % j], 1)
+                v = P["via"].get((j, me))
+                if v is None:
+                    parts.append(([j], uses[me, j], pair(j), place(me), "got"))
+                else:
+                    i = relays[v].index((me, j))
+                    parts.append(([v], uses[me, j], pair(j), T.fwd[:, 4 * i:4 * i + 2], "f%d" % i))
+            send(parts)
+
+    def relay_results():
+        for i, (r, j) in enumerate(relays.get(me, [])):
+            g.wait_ge(S["f%d" % i], len(uses[r, j]))
+            send([([j], engines(me, j), T.fwd[:, 4 * i:4 * i + 2], place(r), "got")])
+
+    g.sync.dma_start(T.xb[:], T.x[:]).then_inc(S["ldx"], 16)
+    g.sync.dma_start(T.wb[:], T.w[:]).then_inc(S["ldw"], 16)
+
+    v = g.vector
+    v.memset(T.low[:], LOW).then_inc(S["low"], 1)
+    v.wait_ge(S["ldx"], 16)
+    v.quantize_mx(T.xq[:, xcols(me)], T.xs[:, xcols(me)], T.xb[:]).then_inc(S["qx"], 1)
+    v.wait_ge(S["ldw"], 16)
+    v.quantize_mx(T.wq[:], T.ws[:], T.wb[:]).then_inc(S["qw"], 1)
+    v.wait_ge(S["low"], 1)
+
+    def kind_of(j):
+        if j == me:
+            return 0
+        if me in entry[j] or me in mates[j]:
+            return 1
+        if lead[j] == me:
+            return 2
+        return 3 if me in far[j] else 4
+
+    g.tensor.wait_ge(S["qx"], 1)
+    g.tensor.wait_ge(S["qw"], 1)
+    for t, j in enumerate(sorted(range(N), key=lambda j: (kind_of(j), j))):
+        landed(g.tensor, "tensor", "s", j)
+        landed(g.tensor, "tensor", "q", j)
+        a = j * PITCH
+        n = NC if t < WHOLE else HALF
+        bank = (t if t < WHOLE else 2 * t - WHOLE) * NC
+        for i in range(NC // n):
+            b = bank + i * NC
+            cols = slice(i * n, (i + 1) * n)
+            last = (i + 1) * n == NC
+            g.tensor.matmul_mx(T.ps[:, b:b + n], T.xq[:, xcols(j)], T.xs[:, xcols(j)], T.wq[:, cols], T.ws[:, cols],
+                               True, True).then_inc(S["mb%d" % j if last else "ma%d" % j], 1)
+            v.wait_ge(S["mb%d" % j if last else "ma%d" % j], 1)
+            if i:
+                v.wait_ge(S["sa%d" % j], 1)
+            v.tensor_tensor_scan(T.pm[:, a + i * n:a + (i + 1) * n], T.ps[:, b:b + n], T.low[:, 0:n],
+                                 T.pm[:, a + i * n - 1:a + i * n] if i else LOW,
+                                 f32max, f32max).then_inc(S["sb%d" % j if last else "sa%d" % j], 1)
+        g.scalar.wait_ge(S["sb%d" % j], 1)
+        g.scalar.activation(T.sgn[:, j * NC:(j + 1) * NC], T.pm[:, a:a + NC], ActivationFunctionType.Sign,
+                            bias=T.pm[:, a + NC - 1:a + NC], scale=-1.0,
+                            accum_out=T.pm[:, a + NC:a + NC + 1]).then_inc(S["sg%d" % j], 1)
+
+    g.iota(T.off[:, 0:N], [[-NC, N]], (N - 1) * NC, 0, allow_small_or_imprecise_dtypes=True).then_inc(S["off"], 1)
+    g.wait_ge(S["qx"], 1)
+    send_tiles()
+    send_results()
+    relay_results()
     g.wait_ge(S["sent"], sent[0])
 
     got = 0
     for r in range(N):
         if r != me:
-            k = kind(r, me)
-            if k == 3:
-                got += len(engines(P["via"][me, r], me))
-            else:
-                got += len(share(r, results(r, k))[me])
+            w = P["via"].get((me, r))
+            got += len(uses[r, me]) if w is None else len(engines(w, me))
     vals = T.res[:, 0:4 * N:4]
     cols = T.res[:, 1:4 * N:4]
-    v = g.vector
     v.wait_ge(S["sg%d" % me], 1)
     v.tensor_copy(place(me), pair(me)).then_inc(S["own"], 1)
     v.wait_ge(S["off"], 1)

from concourse.bass import DstId, RemoteDMATransfer
from concourse.mybir import dt, AluOpType, AxisListType, ActivationFunctionType

N = 5
NC = 512
HALF = NC // 2
WHOLE = 3
TOK = 128
PITCH = NC + 4
LOW = -1.0e29

SCRATCH = {
    "xb": ("sbuf", [128, 4 * TOK], "bfloat16"),
    "wb": ("sbuf", [128, 4 * NC], "bfloat16"),
    "xq": ("sbuf", [128, N * TOK], "float8_e4m3fn_x4"),
    "xs": ("sbuf", [128, N * TOK], "uint8"),
    "wq": ("sbuf", [128, NC], "float8_e4m3fn_x4"),
    "ws": ("sbuf", [128, NC], "uint8"),
    "ps": ("psum", [128, (2 * N - WHOLE) * NC], "float32"),
    "low": ("sbuf", [128, NC], "bfloat16"),
    "pm": ("sbuf", [128, N * PITCH], "float32"),
    "sgn": ("sbuf", [128, N * NC], "bfloat16"),
    "off": ("sbuf", [128, 8], "float32"),
    "res": ("sbuf", [128, 4 * N], "float32"),
    "fwd": ("sbuf", [128, 8], "float32"),
    "idx": ("sbuf", [128, 8], "float32"),
    "neq": ("sbuf", [128, 8], "float32"),
    "fin": ("sbuf", [128, 12], "float32"),
}
SEMAPHORES = (["ldx", "ldw", "qx", "qw", "low", "off", "sent", "got", "own", "m0", "m1", "m2", "done", "stored"]
              + [k + str(j) for k in ("q", "s", "ma", "mb", "sa", "sb", "sg") for j in range(N)] + ["f0", "f1"])


def _bits(mask):
    return [1 << b for b in range(mask.bit_length()) if mask >> b & 1]


def _plan(C, topo):
    R = range(N)
    may = lambda a, b: topo.may_write(C[a], C[b])
    chip = lambda a: (topo.host(C[a]), topo.chip(C[a]))
    rack = lambda a: topo.rack(topo.host(C[a]))
    P = {"far": [], "lead": [], "rest": [], "mates": [], "entry": [], "pass": [], "via": {}}
    for j in R:
        over = [r for r in R if rack(r) != rack(j) and may(j, r)]
        near = {}
        for r in R:
            if rack(r) == rack(j) and chip(r) != chip(j):
                near.setdefault(chip(r), []).append(r)
        P["far"].append([r for r in R if r != j and not may(j, r)])
        P["lead"].append(over[0])
        P["rest"].append([r for r in over[1:] if chip(r) == chip(over[0])])
        P["mates"].append([r for r in R if r != j and chip(r) == chip(j)])
        P["entry"].append([v[-1] for v in near.values()])
        P["pass"].append({v[-1]: v[:-1] for v in near.values() if len(v) > 1})
        for r in P["far"][j]:
            P["via"][j, r] = over[0]
    P["led"] = [[j for j in R if P["lead"][j] == d] for d in R]
    P["order"] = sorted(R, key=lambda j: (P["lead"][j], j))
    return P


def rank_program(g, core, T, topo):
    me = T.rank_of(core)
    if me is None:
        return
    C = T.cores
    P = _plan(C, topo)
    slot = {j: s for s, j in enumerate(P["order"])}
    S = T.sem
    f32max = AluOpType.max
    chip = lambda r: (topo.host(C[r]), topo.chip(C[r]))
    lead, far, rest, mates, entry, passed = (P[k] for k in ("lead", "far", "rest", "mates", "entry", "pass"))

    def engines(a, b, use="all"):
        off = 0xFFFFFFFF
        for d in range(N):
            if d != a and chip(d) != chip(a) and topo.may_write(C[a], C[d]):
                off &= topo.mask(C[a], C[d])
        m = topo.mask(C[a], C[b])
        e = _bits(m & ~off if chip(a) == chip(b) else m & off)
        return {"all": e, "A": e[0::2], "B": e[1::2]}[use]

    def tile_calls(n):
        out = [("s", [n], [lead[n]], "A"), ("q", [n], [lead[n]], "A"),
               ("s", [n], entry[n] + mates[n], "B"), ("q", [n], entry[n] + mates[n], "B")]
        groups = {}
        for j in P["order"]:
            if lead[j] == n:
                groups.setdefault(tuple(far[j] + rest[j]), []).append(j)
        for ds, ts in groups.items():
            out.append(("s", ts, list(ds), "all"))
            out += [("q", [j], list(ds), "all") for j in ts]
        for j in range(N):
            if n in passed[j]:
                out += [("s", [j], passed[j][n], "all"), ("q", [j], passed[j][n], "all")]
        return out

    arrive = {}
    for n in range(N):
        for kind, ts, ds, use in tile_calls(n):
            for d in ds:
                for j in ts:
                    arrive[d, kind, j] = (kind + str(ts[0]), len(engines(n, d, use)))

    sent = [0]

    def send(parts):
        for p in parts:
            sent[0] += len(p[1])
        if len(parts) == 1 and len(parts[0][0]) == 1:
            (d,), e, src, dst, sem = parts[0]
            rid, pid = topo.addr(C[d], core)
            g.remote_dma(dst, src, S[sem], S["sent"], pid, rid, sum(e))
            return
        tr = []
        for ds, e, src, dst, sem in parts:
            ids = [DstId(rid=a[0], pnc=a[1]) for a in (topo.addr(C[d], core) for d in ds)]
            tr.append(RemoteDMATransfer(dst_ids=ids, dma_engine_mask=sum(e), remote_sem=S[sem],
                                        srcs=[src], dsts=[dst] * len(ds)))
        g.remote_dma_fused(tr, local_sem=S["sent"])

    seen = {"g": set(), "tensor": set()}

    def landed(queue, name, kind, j):
        if j != me and arrive[me, kind, j][0] not in seen[name]:
            seen[name].add(arrive[me, kind, j][0])
            queue.wait_ge(S[arrive[me, kind, j][0]], arrive[me, kind, j][1])

    def xcols(j):
        return slice(slot[j] * TOK, (slot[j] + 1) * TOK)

    def send_tiles():
        for kind, ts, ds, use in tile_calls(me):
            for j in ts:
                landed(g, "g", kind, j)
            a = min(slot[j] for j in ts) * TOK
            b = a + len(ts) * TOK
            v = T.xq[:, a:b].bitcast(dt.uint8) if kind == "q" else T.xs[:, a:b]
            away = [d for d in ds if chip(d) != chip(me)]
            here = [d for d in ds if chip(d) == chip(me)]
            send([(part, engines(me, part[0], use), v, v, kind + str(ts[0])) for part in (away, here) if part])

    def result_calls(r):
        a = P["led"][r]
        f = [j for j in range(N) if r in far[j]]
        return [js for js in [a] + [[j] for j in f] + [[j for j in range(N) if j != r and j not in a + f]] if js]

    def share(r, js):
        hop = {j: P["via"].get((j, r), j) for j in js}
        here = [j for j in js if chip(hop[j]) == chip(r)]
        out = {}
        for part in (here, [j for j in js if j not in here]):
            if part:
                e = engines(r, hop[part[0]])
                n = len(e)
                while n * len(part) > len(e):
                    n //= 2
                for i, j in enumerate(part):
                    out[j] = e[i * n:(i + 1) * n]
        return out

    uses = {(r, j): e for r in range(N) for js in result_calls(r) for j, e in share(r, js).items()}
    relays = {}
    for (j, r), v in sorted(P["via"].items()):
        relays.setdefault(v, []).append((r, j))

    def pair(j):
        return T.pm[:, j * PITCH + NC - 1:j * PITCH + NC + 1]

    def place(r):
        return T.res[:, 4 * (N - 1 - r):4 * (N - 1 - r) + 2]

    def send_results():
        for js in result_calls(me):
            parts = []
            for j in js:
                g.wait_ge(S["sg%d" % j], 1)
                v = P["via"].get((j, me))
                if v is None:
                    parts.append(([j], uses[me, j], pair(j), place(me), "got"))
                else:
                    i = relays[v].index((me, j))
                    parts.append(([v], uses[me, j], pair(j), T.fwd[:, 4 * i:4 * i + 2], "f%d" % i))
            send(parts)

    def relay_results():
        for i, (r, j) in enumerate(relays.get(me, [])):
            g.wait_ge(S["f%d" % i], len(uses[r, j]))
            send([([j], engines(me, j), T.fwd[:, 4 * i:4 * i + 2], place(r), "got")])

    g.sync.dma_start(T.xb[:], T.x[:]).then_inc(S["ldx"], 16)
    g.sync.dma_start(T.wb[:], T.w[:]).then_inc(S["ldw"], 16)

    v = g.vector
    v.memset(T.low[:], LOW).then_inc(S["low"], 1)
    v.wait_ge(S["ldx"], 16)
    v.quantize_mx(T.xq[:, xcols(me)], T.xs[:, xcols(me)], T.xb[:]).then_inc(S["qx"], 1)
    v.wait_ge(S["ldw"], 16)
    v.quantize_mx(T.wq[:], T.ws[:], T.wb[:]).then_inc(S["qw"], 1)
    v.wait_ge(S["low"], 1)

    def kind_of(j):
        if j == me:
            return 0
        if me in entry[j] or me in mates[j]:
            return 1
        if lead[j] == me:
            return 2
        return 3 if me in far[j] else 4

    g.tensor.wait_ge(S["qx"], 1)
    g.tensor.wait_ge(S["qw"], 1)
    for t, j in enumerate(sorted(range(N), key=lambda j: (kind_of(j), j))):
        landed(g.tensor, "tensor", "s", j)
        landed(g.tensor, "tensor", "q", j)
        a = j * PITCH
        n = NC if t < WHOLE else HALF
        bank = (t if t < WHOLE else 2 * t - WHOLE) * NC
        for i in range(NC // n):
            b = bank + i * NC
            cols = slice(i * n, (i + 1) * n)
            last = (i + 1) * n == NC
            g.tensor.matmul_mx(T.ps[:, b:b + n], T.xq[:, xcols(j)], T.xs[:, xcols(j)], T.wq[:, cols], T.ws[:, cols],
                               True, True).then_inc(S["mb%d" % j if last else "ma%d" % j], 1)
            v.wait_ge(S["mb%d" % j if last else "ma%d" % j], 1)
            if i:
                v.wait_ge(S["sa%d" % j], 1)
            v.tensor_tensor_scan(T.pm[:, a + i * n:a + (i + 1) * n], T.ps[:, b:b + n], T.low[:, 0:n],
                                 T.pm[:, a + i * n - 1:a + i * n] if i else LOW,
                                 f32max, f32max).then_inc(S["sb%d" % j if last else "sa%d" % j], 1)
        g.scalar.wait_ge(S["sb%d" % j], 1)
        g.scalar.activation(T.sgn[:, j * NC:(j + 1) * NC], T.pm[:, a:a + NC], ActivationFunctionType.Sign,
                            bias=T.pm[:, a + NC - 1:a + NC], scale=-1.0,
                            accum_out=T.pm[:, a + NC:a + NC + 1]).then_inc(S["sg%d" % j], 1)

    g.iota(T.off[:, 0:N], [[-NC, N]], (N - 1) * NC, 0, allow_small_or_imprecise_dtypes=True).then_inc(S["off"], 1)
    g.wait_ge(S["qx"], 1)
    send_tiles()
    send_results()
    relay_results()
    g.wait_ge(S["sent"], sent[0])

    got = 0
    for r in range(N):
        if r != me:
            w = P["via"].get((me, r))
            got += len(uses[r, me]) if w is None else len(engines(w, me))
    vals = T.res[:, 0:4 * N:4]
    cols = T.res[:, 1:4 * N:4]
    v.wait_ge(S["sg%d" % me], 1)
    v.tensor_copy(place(me), pair(me)).then_inc(S["own"], 1)
    v.wait_ge(S["off"], 1)
    v.wait_ge(S["own"], 1)
    v.wait_ge(S["got"], got)
    v.tensor_reduce(T.fin[:, 7:8], vals, AxisListType.X, f32max).then_inc(S["m0"], 1)
    v.tensor_tensor(T.idx[:, 0:N], cols, T.off[:, 0:N], AluOpType.add).then_inc(S["m1"], 1)
    v.wait_ge(S["m0"], 1)
    v.tensor_scalar(T.neq[:, 0:N], vals, T.fin[:, 7:8], None, AluOpType.is_lt).then_inc(S["m2"], 1)
    v.wait_ge(S["m1"], 1)
    v.wait_ge(S["m2"], 1)
    v.tensor_tensor_scan(T.fin[:, 0:10:2], T.neq[:, 0:N], T.idx[:, 0:N], 0.0, AluOpType.mult, f32max).then_inc(S["done"], 1)
    g.sync.wait_ge(S["done"], 1)
    g.sync.dma_start(T.y[:], T.fin[:, 7:9]).then_inc(S["stored"], 16)
    g.sync.wait_ge(S["stored"], 16)
